import numpy as np
CORES = [33,34,161,162,289,290,417,418]
N = 8
T, FF, CAP, CAPP = 2048, 2, 512, 128
def entries(a): return a.T.reshape(-1)
def pack(v, P): return np.ascontiguousarray(np.asarray(v, np.int32).reshape(-1, P).T)
def lists(rng, how):
    O = np.stack([rng.permutation(np.repeat(np.arange(N), CAPP))[:CAP] for k in range(N)])
    if how == "apart": s = int(rng.integers(N * CAPP - CAP + 1)); cnt = np.bincount(np.repeat(np.arange(N), CAPP)[s:s + CAP], minlength=N); a = rng.permutation(N); O = np.stack([rng.permutation(np.repeat(np.arange(N), cnt[(a + k) % N])) for k in rng.permutation(N)])
    if how == "full": z = rng.permutation(N); O = np.stack([rng.permutation(np.repeat(z, CAPP)[:CAP]) for k in range(N)])
    if how == "none": z = int(rng.integers(N)); O = np.stack([rng.permutation(np.repeat(np.delete(np.arange(N), z), CAPP))[:CAP] for k in range(N)])
    P = np.zeros((N, CAP), np.int64)
    for o in range(N):
        q = rng.permutation(T); u = 0
        for k in range(N):
            m = np.nonzero(O[k] == o)[0]
            if how != "apart": q = rng.permutation(T); u = 0
            if how == "sorted": q = np.r_[0, T - 1, 1 + rng.permutation(T - 2)]
            P[k, m] = T * o + q[u:u + len(m)]; u += len(m)
    if how == "same": P = np.stack([rng.permutation(P[0]) for k in range(N)])
    if how == "sorted": P = np.sort(P, axis=1)
    G = 2 * rng.random((N, 16, CAP // 16), dtype=np.float32) - 1
    if how == "none": G[rng.random(G.shape) < 0.125] = 0
    return {"gate": G, "pick": np.stack([pack(p, 16) for p in P])}
def setup_inputs(rng):
    return dict({"x": rng.standard_normal((N, 128, T), dtype=np.float32), "w1": (rng.standard_normal((N, 128, FF * 128), dtype=np.float32) / 8), "w2": (rng.standard_normal((N, 128, FF * 128), dtype=np.float32) / 16)}, **lists(rng, "uniform"))
def setup_inputs_apart(rng):
    d = setup_inputs(rng); d.update(lists(rng, "apart"))
    for k in ("x",): d[k] = (d[k].astype(np.float32) * 1024.0).astype(d[k].dtype)
    return d
def setup_inputs_full(rng):
    d = setup_inputs(rng); d.update(lists(rng, "full"))
    for k in ("x",): d[k] = (d[k].astype(np.float32) * (1 / 1024.0)).astype(d[k].dtype)
    return d
def setup_inputs_none(rng):
    d = setup_inputs(rng); d.update(lists(rng, "none"))
    return d
def setup_inputs_same(rng):
    d = setup_inputs(rng); d.update(lists(rng, "same"))
    return d
def setup_inputs_sorted(rng):
    d = setup_inputs(rng); d.update(lists(rng, "sorted"))
    return d
def check_inputs(x):
    bad = []
    if x["pick"].min() < 0 or x["pick"].max() >= N * T: bad.append("pick out of range")
    if any(len(np.unique(a)) != a.size for a in x["pick"]): bad.append("a token stands twice in a list")
    if max(int(np.bincount(entries(a) // T, minlength=N).max()) for a in x["pick"]) > CAPP: bad.append("more than CAPP of an expert's tokens lie on one rank")
    return bad
def reference(x, w1, w2, gate, pick):
    X, W1, W2 = x.astype(np.float64), w1.astype(np.float64), w2.astype(np.float64)
    A = np.concatenate(list(X), axis=1); Y = np.zeros((128, N * T))
    for k in range(N):
        P = entries(pick[k]); g = entries(gate[k]).astype(np.float64)
        Y[:, P] += g[None, :] * sum(W2[k][:, 128 * f:128 * f + 128].T @ np.maximum(W1[k][:, 128 * f:128 * f + 128].T @ A[:, P], 0.0) for f in range(FF))
    return {"y": np.stack([Y[:, T * r:T * r + T] for r in range(N)]).astype(np.float32)}

from concourse.bass import DstId, RemoteDMATransfer
from concourse.mybir import AluOpType, AxisListType, ActivationFunctionType

NR, TOK, CAPP = 8, 2048, 128
TW = TOK + CAPP
CA, WW = 256, 528
LT = 512

SCRATCH = {
    "xw": ("sbuf", [128, TW], "float32"),
    "yw": ("sbuf", [128, TW], "float32"),
    "pk": ("sbuf", [128, 4], "int32"), "gt": ("sbuf", [128, 4], "float32"),
    "dsi": ("sbuf", [128, 4], "int32"), "toi": ("sbuf", [128, 4], "int32"),
    "dsf": ("sbuf", [128, 4], "float32"), "tom": ("sbuf", [128, 4], "float32"),
    "slf": ("sbuf", [128, 4], "float32"), "val": ("sbuf", [128, 4], "float32"),
    "ez": ("sbuf", [128, 56], "float32"), "ec": ("sbuf", [128, 32], "float32"),
    "oneh": ("sbuf", [128, 512], "float32"), "rl": ("sbuf", [128, 64], "float32"),
    "io128": ("sbuf", [128, 128], "float32"), "iomod": ("sbuf", [128, 128], "float32"),
    "pif": ("sbuf", [128, 1], "float32"), "pii": ("sbuf", [128, 1], "int32"),
    "pad": ("sbuf", [128, 1], "float32"),
    "pmi": ("sbuf", [128, 1], "int32"), "pdi": ("sbuf", [128, 1], "int32"),
    "pmf": ("sbuf", [128, 1], "float32"), "pdf": ("sbuf", [128, 1], "float32"),
    "tri": ("sbuf", [128, 128], "float32"), "ones": ("sbuf", [128, 128], "float32"),
    "eye": ("sbuf", [128, 128], "float32"), "mod": ("sbuf", [128, 128], "float32"),
    "m8": ("sbuf", [128, 8], "float32"),
    "r8": ("sbuf", [128, 64], "float32"), "offs": ("sbuf", [128, 64], "uint16"),
    "dg": ("sbuf", [128, 1024], "float32"), "gb": ("sbuf", [128, 1024], "float32"),
    "vg": ("sbuf", [128, 1024], "float32"), "hs": ("sbuf", [128, 2048], "float32"),
    "t1": ("sbuf", [128, 1024], "float32"), "t2": ("sbuf", [128, 1024], "float32"),
}
for _k in range(NR):
    SCRATCH["wt%d" % _k] = ("sbuf", [128, WW], "float32")
for _n in ("pc", "pl", "po", "pg", "ph0", "ph1", "py0", "py1"):
    SCRATCH[_n] = ("psum", [128, 512], "float32")

SEMAPHORES = ["lp", "lg", "l1", "l2", "lx", "xgo", "sent", "stored", "sv", "sp", "ss", "sg"]
SEMAPHORES += ["a%d" % _k for _k in range(NR)] + ["b%d" % _k for _k in range(NR)]


def rank_program(g, core, T, topo):
    rank = T.rank_of(core)
    if rank is None:
        return
    cores = list(T.cores)
    OP, AF = AluOpType, ActivationFunctionType
    sem = T.sem

    def place(c):
        return [d for d in cores if topo.host(d) == topo.host(c) and topo.chip(d) == topo.chip(c)]
    lane = place(core).index(core)
    other = [d for d in place(core) if d != core][0]
    planes = [d for d in cores if topo.same_plane(core, d)]
    cables = [d for d in cores if topo.rack(topo.host(d)) != topo.rack(topo.host(core)) and topo.may_write(core, d)]
    diags = [d for d in cores if d != core and not topo.may_write(core, d)]
    plane = [d for d in planes if place(d).index(d) == lane][0]
    cable = [d for d in cables if place(d).index(d) == lane][0]
    diag = [d for d in diags if place(d).index(d) == lane][0]
    rk = T.rank_of

    off = topo.mask(core, plane) & topo.mask(core, cable)
    on = topo.mask(core, other)
    on2 = on & ~off

    def did(d):
        rid, pid = topo.addr(d, core)
        return DstId(rid=rid, pnc=pid)

    cnt = {"sv": 0, "sp": 0, "ss": 0, "sg": 0}
    Q = {"sv": g.vector, "sp": g.tensor, "ss": g.scalar, "sg": g, "sy": g.sync}
    seen = {q: {} for q in Q}

    def need(q, deps):
        for d in deps:
            if d is None:
                continue
            s, n = d
            if seen[q].get(s, 0) < n:
                Q[q].wait_ge(sem[s], n)
                seen[q][s] = n

    def emit(q, f, deps=()):
        need(q, deps)
        f().then_inc(sem[q], 1)
        cnt[q] += 1
        return (q, cnt[q])

    def V(f, *deps): return emit("sv", f, deps)
    def P(f, *deps): return emit("sp", f, deps)
    def S(f, *deps): return emit("ss", f, deps)
    def G(f, *deps): return emit("sg", f, deps)
    vec, pe, sc = g.vector, g.tensor, g.scalar
    W = [T["wt%d" % k] for k in range(NR)]
    own = W[rank]

    sc.dma_start(T.pk[:], T.pick[:]).then_inc(sem.lp, 16)
    sc.dma_start(T.gt[:], T.gate[:]).then_inc(sem.lg, 16)
    g.sync.dma_start(own[:, 0:CA], T.w1[:]).then_inc(sem.l1, 16)
    g.sync.dma_start(own[:, CA:LT], T.w2[:]).then_inc(sem.l2, 16)
    lp, lg, l1, l2, lx = ("lp", 16), ("lg", 16), ("l1", 16), ("l2", 16), ("lx", 16)

    k_io = G(lambda: g.iota(T.io128[:], [[1, 128]], 0, 0, allow_small_or_imprecise_dtypes=True))
    k_pf = G(lambda: g.iota(T.pif[:], [[0, 1]], 0, 1, allow_small_or_imprecise_dtypes=True))
    k_pd = G(lambda: g.iota(T.pad[:], [[0, 1]], TOK, 1, allow_small_or_imprecise_dtypes=True))
    k_pi = G(lambda: g.iota(T.pii[:], [[0, 1]], 0, 1))
    k_im = G(lambda: g.iota(T.iomod[:], [[0, 8], [1, 16]], 0, 0, allow_small_or_imprecise_dtypes=True))
    v_ez = V(lambda: vec.memset(T.ez[:, 0:24], 0.0))
    v_on = V(lambda: vec.memset(T.ones[:], 1.0))
    v_xp = V(lambda: vec.memset(T.xw[:, TOK:TW], 0.0))
    v_y0 = V(lambda: vec.memset(T.yw[:, 0:TW // 2], 0.0))
    v_tri = V(lambda: vec.tensor_scalar(T.tri[:], T.io128[:], T.pif[:, 0:1], None, OP.is_gt), k_io, k_pf)

    v_ds = V(lambda: vec.tensor_scalar(T.dsi[:], T.pk[:], 11, None, OP.arith_shift_right), lp)
    v_to = V(lambda: vec.tensor_scalar(T.toi[:], T.pk[:], TOK - 1, None, OP.bitwise_and))
    v_df = V(lambda: vec.tensor_copy(T.dsf[:], T.dsi[:]), v_ds)
    v_tm = V(lambda: vec.tensor_scalar(T.tom[:], T.toi[:], float(-TOK), None, OP.add), v_to)
    v_e = None
    for c in range(4):
        v_e = V(lambda: vec.tensor_scalar(T.ez[:, 24 + 8 * c:32 + 8 * c], T.io128[:, 0:8], T.dsf[:, c:c + 1], None,
                                          OP.is_equal), v_df, k_io)
    P(lambda: pe.matmul(T.pc[:, 0:32], T.tri[:], T.ez[:, 24:56], True, False), v_e, v_tri, v_ez, v_on)
    P(lambda: pe.matmul(T.pc[:, 0:32], T.ones[:], T.ez[:, 16:48], False, False))
    P(lambda: pe.matmul(T.pc[:, 0:32], T.ones[:], T.ez[:, 8:40], False, False))
    p_c = P(lambda: pe.matmul(T.pc[:, 0:32], T.ones[:], T.ez[:, 0:32], False, True))
    s_rl = None
    for c in range(4):
        s_rl = S(lambda: sc.activation(T.rl[:, 16 * c + 8:16 * c + 16], T.ez[:, 24 + 8 * c:32 + 8 * c], AF.Copy, 0.0,
                                       T.gt[:, c:c + 1]), v_e, lg)
    v_pm = V(lambda: vec.tensor_scalar(T.pmi[:], T.pii[:], 15, None, OP.bitwise_and), k_pi)
    v_pq = V(lambda: vec.tensor_scalar(T.pdi[:], T.pii[:], 4, None, OP.arith_shift_right))
    v_ec = V(lambda: vec.tensor_tensor(T.ec[:], T.ez[:, 24:56], T.pc[:, 0:32], OP.mult), p_c, v_e)
    v_sl = None
    for c in range(4):
        v_sl = V(lambda: vec.tensor_reduce(T.slf[:, c:c + 1], T.ec[:, 8 * c:8 * c + 8], AxisListType.X, OP.add), v_ec)
    v_va = V(lambda: vec.tensor_tensor(T.val[:], T.tom[:], T.slf[:], OP.subtract), v_sl, v_tm)
    v_oh = []
    for c in range(4):
        V(lambda: vec.tensor_scalar(T.oneh[:, 128 * c:128 * c + 128], T.io128[:], T.slf[:, c:c + 1], None, OP.is_equal),
          v_sl)
        v_oh.append(V(lambda: vec.tensor_scalar(T.rl[:, 16 * c:16 * c + 8], T.ez[:, 24 + 8 * c:32 + 8 * c],
                                                T.val[:, c:c + 1], None, OP.mult), v_va))
    p_l = None
    for c in range(4):
        p_l = P(lambda: pe.matmul(T.pl[:, 0:16], T.oneh[:, 128 * c:128 * c + 128], T.rl[:, 16 * c:16 * c + 16],
                                  c == 0, c == 3), v_oh[c], s_rl)
    v_l0 = V(lambda: vec.tensor_scalar(own[:, LT:LT + 8], T.pl[:, 0:8], T.pad[:, 0:1], None, OP.add), p_l, k_pd)
    v_lt = V(lambda: vec.tensor_copy(own[:, LT + 8:LT + 16], T.pl[:, 8:16]))

    V(lambda: vec.tensor_copy(T.pmf[:], T.pmi[:]), v_pm)
    v_pf = V(lambda: vec.tensor_copy(T.pdf[:], T.pdi[:]), v_pq)
    v_m8 = V(lambda: vec.tensor_scalar(T.m8[:], T.io128[:, 0:8], T.pdf[:, 0:1], None, OP.is_equal), v_pf)
    v_mod = V(lambda: vec.tensor_scalar(T.mod[:], T.iomod[:], T.pmf[:, 0:1], None, OP.is_equal), k_im)
    v_eye = V(lambda: vec.tensor_scalar(T.eye[:], T.io128[:], T.pif[:, 0:1], None, OP.is_equal))

    sent = [0]

    def send(parts, deps):
        need("sg", deps)
        ts = []
        for dsts, mask, k, part in parts:
            lo, hi = (0, CA) if part == "a" else (CA, WW)
            ts.append(RemoteDMATransfer(dst_ids=[did(d) for d in dsts], dma_engine_mask=mask, remote_sem=sem[part + str(k)],
                                        srcs=[W[k][:, lo:hi]], dsts=[W[k][:, lo:hi] for d in dsts]))
            sent[0] += bin(mask).count("1")
        g.remote_dma_fused(ts, local_sem=sem.sent)

    noff, non, non2 = bin(off).count("1"), bin(on).count("1"), bin(on2).count("1")
    kp, kc, kd = rk(plane), rk(cable), rk(diag)
    op_, oc_, od_ = [rk([d for d in place(m) if d != m][0]) for m in (plane, cable, diag)]
    oo = rk(other)
    arr = {}
    for k in (kp, kc, kd):
        for part in "ab":
            arr[(k, part)] = (part + str(k), noff)
    arr[(rank, "a")], arr[(rank, "b")] = l1, v_lt
    for k, part, n in ((oo, "a", non2), (oo, "b", non2), (op_, "a", non2), (oc_, "b", non2),
                       (oc_, "a", non), (op_, "b", non), (od_, "a", non), (od_, "b", non)):
        arr[(k, part)] = (part + str(k), n)

    send([([plane, cable], off, rank, "a"), ([other], on2, rank, "a")], [l1])
    g.sem_inc(sem.xgo, 1)
    send([([plane, cable], off, rank, "b"), ([other], on2, rank, "b")], [l2, v_lt])
    send([([cable], off, kp, "a"), ([other], on2, kp, "a")], [arr[(kp, "a")]])
    send([([other], on, kc, "a")], [arr[(kc, "a")]])
    send([([plane], off, kc, "b"), ([other], on2, kc, "b")], [arr[(kc, "b")]])
    send([([other], on, kp, "b")], [arr[(kp, "b")]])
    send([([other], on, kd, "a")], [arr[(kd, "a")]])
    send([([other], on, kd, "b")], [arr[(kd, "b")]])

    g.sync.wait_ge(sem.xgo, 1)
    g.sync.dma_start(T.xw[:, 0:TOK], T.x[:]).then_inc(sem.lx, 16)

    stages = [[rank, oo], [kp, kc], [op_, oc_], [kd], [od_]]
    NS = len(stages)
    base, b0 = [], 0
    for s in stages:
        base.append(b0)
        b0 += len(s)
    vy = [v_y0]
    st = [dict() for s in stages]
    prev = {}

    def prep_v1(j):
        d = st[j]
        for i, k in enumerate(stages[j]):
            o = 8 * (base[j] + i)
            d["r8"] = V(lambda: vec.tensor_scalar(T.r8[:, o:o + 8], T.m8[:], W[k][:, LT + rank:LT + rank + 1], None, OP.mult),
                        arr[(k, "b")], v_m8)

    def prep_s(j):
        d = st[j]
        for i, k in enumerate(stages[j]):
            o = 128 * (base[j] + i)
            d["dg"] = S(lambda: sc.activation(T.dg[:, o:o + 128], T.eye[:], AF.Copy, 0.0,
                                              W[k][:, LT + 8 + rank:LT + 9 + rank]), arr[(k, "b")], v_eye)

    def prep_p(j):
        d, n, o = st[j], len(stages[j]), base[j]
        d["po"] = P(lambda: pe.matmul(T.po[:, 0:8 * n], T.mod[:], T.r8[:, 8 * o:8 * (o + n)], True, True),
                    d["r8"], v_mod, prev.get("po"))
        d["pg"] = P(lambda: pe.matmul(T.pg[:, 0:128 * n], T.ones[:], T.dg[:, 128 * o:128 * (o + n)], True, True),
                    d["dg"], v_on, prev.get("pg"))

    def prep_v2(j):
        d, n, o = st[j], len(stages[j]), base[j]
        d["off"] = V(lambda: vec.tensor_copy(T.offs[:, 8 * o:8 * (o + n)], T.po[:, 0:8 * n]), d["po"])
        prev["po"] = d["off"]

    def gather_s(j):
        d, n, o = st[j], len(stages[j]), base[j]
        d["vg"] = S(lambda: sc.activation(T.vg[:, 128 * o:128 * (o + n)],
                                          T.xw[:, 0:TW].indirect(T.offs[:, 8 * o:8 * (o + n)]), AF.Copy), d["off"], lx, v_xp)
        d["gb"] = S(lambda: sc.activation(T.gb[:, 128 * o:128 * (o + n)], T.pg[:, 0:128 * n], AF.Copy), d["pg"])
        prev["pg"] = d["gb"]

    def layer1(j):
        d = st[j]
        for i, k in enumerate(stages[j]):
            o = base[j] + i
            ph = T["ph%d" % (o % 2)]
            for f in range(2):
                d["h%d" % i] = P(lambda: pe.matmul(ph[:, 128 * f:128 * f + 128], W[k][:, 128 * f:128 * f + 128],
                                                   T.vg[:, 128 * o:128 * o + 128], True, True),
                                 d["vg"], arr[(k, "a")], prev.get("ph%d" % (o % 2)))

    def relu(j):
        d = st[j]
        for i, k in enumerate(stages[j]):
            o = base[j] + i
            d["r%d" % i] = S(lambda: sc.activation(T.hs[:, 256 * o:256 * o + 256], T["ph%d" % (o % 2)][:, 0:256], AF.Relu),
                             d["h%d" % i])
            prev["ph%d" % (o % 2)] = d["r%d" % i]

    def layer2(j):
        d = st[j]
        for i, k in enumerate(stages[j]):
            o = base[j] + i
            py = T["py%d" % (o % 2)]
            dw = l2 if k == rank else arr[(k, "b")]
            for f in range(2):
                d["y%d" % i] = P(lambda: pe.matmul(py[:, 0:128], W[k][:, CA + 128 * f:CA + 128 * f + 128],
                                                   T.hs[:, 256 * o + 128 * f:256 * o + 128 * f + 128], f == 0, f == 1),
                                 d["r%d" % i], dw, prev.get("py%d" % (o % 2)))

    def combine(j):
        d = st[j]
        for i, k in enumerate(stages[j]):
            o = base[j] + i
            c0, c1 = 128 * o, 128 * o + 128
            a = V(lambda: vec.tensor_tensor(T.t1[:, c0:c1], T["py%d" % (o % 2)][:, 0:128], T.gb[:, c0:c1], OP.mult),
                  d["y%d" % i], d["gb"])
            prev["py%d" % (o % 2)] = a
            src = T.t1
            if o > 0:
                a = V(lambda: vec.tensor_tensor(T.t2[:, c0:c1], T.yw[:, 0:TW].indirect(T.offs[:, 8 * o:8 * o + 8]),
                                                T.t1[:, c0:c1], OP.add), a, vy[0])
                src = T.t2
            vy[0] = V(lambda: vec.tensor_copy(T.yw[:, 0:TW].indirect(T.offs[:, 8 * o:8 * o + 8]), src[:, c0:c1]), a, vy[0])

    for j in range(NS):
        prep_v1(j)
        prep_s(j)
        prep_p(j)
        prep_v2(j)
        gather_s(j)
        if j == 0:
            vy[0] = V(lambda: vec.memset(T.yw[:, TW // 2:TW], 0.0))
        else:
            combine(j - 1)
        layer1(j)
        relu(j)
        layer2(j)
    combine(NS - 1)

    need("sy", [vy[0]])
    g.sync.dma_start(T.y[:], T.yw[:, 0:TOK]).then_inc(sem.stored, 16)
    g.sync.wait_ge(sem.stored, 16)
    need("sy", [("sp", cnt["sp"]), ("ss", cnt["ss"]), ("sg", cnt["sg"])])
    g.wait_ge(sem.sent, sent[0])
